import numpy as np
import ml_dtypes


def mxq(x, axis, fmt="e4m3"):
    dtype, down = {"e4m3": (ml_dtypes.float8_e4m3fn, 7), "e5m2": (ml_dtypes.float8_e5m2, 14)}[fmt]
    v = np.moveaxis(np.asarray(x, np.float32).astype(ml_dtypes.bfloat16).astype(np.float64), axis, -1)
    blocks = v.reshape(v.shape[:-1] + (-1, 32))
    amax = np.abs(blocks).max(-1, keepdims=True)
    byte = np.maximum(np.where(amax > 0, np.frexp(amax)[1] - 1 + 127, 0) - down, 1)
    scale = np.exp2(byte - 127.0)
    codes = (blocks / scale).astype(np.float32).astype(dtype).astype(np.float64)
    return np.moveaxis((codes * scale).reshape(v.shape), -1, axis)


WIDE = False


def mx_kscale(k):
    if not WIDE:
        return np.ones(k)
    levels = np.array([10, -10, 5, -5, 0])
    if k % 512:
        return np.exp2(np.random.permutation(np.resize(levels, k // 32))).repeat(32)
    a = np.empty((k // 512, 16))
    for p in range(k // 512):
        a[p, :8] = np.random.permutation(np.resize(levels, 8))
        for g in range(8):
            far = levels[np.abs(levels - a[p, g]) >= 10]
            a[p, g + 8] = far[np.random.randint(len(far))]
    return np.exp2(a.ravel()).repeat(32)


def f64(x):
    return np.asarray(x).astype(np.float64)


def striped(idx):
    return np.tile(idx.reshape(-1, 16).T, (8, 1)).astype(np.uint16)


def unstriped(offs):
    return offs[:16].T.reshape(-1).astype(np.int64)


def striped8(idx):
    return np.concatenate([x.reshape(-1, 16).T for x in idx]).astype(np.uint16)


def runs(offs, k):
    lists = np.stack([offs[16 * r : 16 * r + 16].T.reshape(-1) for r in range(8)]).astype(np.int64)
    return lists[np.arange(k) % 512 // 64]


def pack_weight(w):
    k, n = w.shape
    w = f64(np.asarray(w, np.float32).astype(ml_dtypes.bfloat16)).reshape(k // 32, 32, n)
    amax = np.abs(w).max(1)
    byte = np.clip(np.where(amax > 0, np.frexp(amax)[1] - 1 + 127 - 7, 1), 1, 254)
    scaled = (w * np.exp2(127.0 - byte)[:, None, :]).reshape(k, n).astype(np.float32)
    words = np.ascontiguousarray(scaled.reshape(k // 512, 128, 4, n).transpose(0, 1, 3, 2)).astype(ml_dtypes.float8_e4m3fn).view(np.uint8)
    return words, np.ascontiguousarray(byte.astype(np.uint8).reshape(k // 512, 16, n))


def unpack_weight(words, scales):
    g, p, n, _ = words.shape
    vals = np.ascontiguousarray(words).view(ml_dtypes.float8_e4m3fn).astype(np.float64) * np.repeat(np.exp2(scales.astype(np.float64) - 127.0), 8, axis=1)[..., None]
    return vals.transpose(0, 1, 3, 2).reshape(g * 512, n)

def planes(y):
    n, m = y.shape
    v = y.astype(np.float32).astype(ml_dtypes.bfloat16).astype(np.float64).reshape(n // 32, 32, m)
    top = np.abs(v).max(1)
    byte = np.clip(np.where(top > 0, np.frexp(top)[1] - 1 + 127 - 7, 1), 1, 254)
    codes = (v * np.exp2(127.0 - byte)[:, None, :]).reshape(n, m).astype(np.float32).astype(ml_dtypes.float8_e4m3fn).view(np.uint8)
    words = codes.reshape(n // 512, 128, 4, m).transpose(0, 1, 3, 2)
    return np.ascontiguousarray(words), np.ascontiguousarray(byte.astype(np.uint8).reshape(n // 512, 16, m))


K, T, S, H, G, U = 512, 1024, 512, 512, 2048, 1024


def setup_inputs():
    n = np.random.standard_normal
    s = mx_kscale(K)[:, None]
    packed_xT = pack_weight(n((K, T)) * s)
    packed_w1 = pack_weight(n((K, H)) / np.sqrt(K) / s)
    packed_w2 = pack_weight(n((K, H)) / np.sqrt(K) / s)
    packed_dT = pack_weight(n((K, G)) / s)
    return {
        "x_words": packed_xT[0],
        "x_scales": packed_xT[1],
        "w1_words": packed_w1[0],
        "w1_scales": packed_w1[1],
        "w2_words": packed_w2[0],
        "w2_scales": packed_w2[1],
        "gs": (np.random.uniform(0.5, 1.5, (K, 1)) * s).astype(np.float32),
        "d_words": packed_dT[0],
        "d_scales": packed_dT[1],
        "mem": n((H, U)).astype(np.float32),
        "offs": striped(np.random.permutation(T)[:S]),
        "two": striped(np.random.permutation(T)[:S]),
        "n1": striped8(np.stack([np.random.permutation(S) for _ in range(8)])),
        "n2": striped8(np.stack([np.random.permutation(S) for _ in range(8)])),
        "k1": striped8(np.random.randint(0, G, (8, H))),
        "n3": striped8(np.stack([np.random.permutation(U)[:S] for _ in range(8)])),
    }


def reference(x_words, x_scales, w1_words, w1_scales, w2_words, w2_scales, gs, d_words, d_scales, mem, offs, two, n1, n2, k1, n3):
    d_k1 = unpack_weight(d_words, d_scales)[np.arange(K)[:, None], runs(k1, K)]
    xq = unpack_weight(x_words, x_scales)[:, unstriped(offs)]
    y = unpack_weight(w1_words, w1_scales).T @ xq
    x_two = unpack_weight(x_words, x_scales)[:, unstriped(two)]
    d = unpack_weight(w2_words, w2_scales).T @ x_two
    z = f64(gs) * (y * (np.tanh(d[np.arange(H)[:, None], runs(n1, H)] - (d[np.arange(H)[:, None], runs(n2, H)]))))
    h = 0.0625 * ((d_k1.T @ mxq(z, 0, "e4m3")))
    nw = np.maximum(h, 0.5 * (f64(mem)[np.arange(H)[:, None], runs(n3, H)]))
    out = f64(mem).copy()
    out[np.arange(H)[:, None], runs(n3, H)] = nw
    return (out,) + planes(out)

@@ -1,0 +1,227 @@
+from contextlib import ExitStack
+
+import concourse.mybir as mybir
+
+K, T, S, H, G, U = 512, 1024, 512, 512, 2048, 1024
+FLOPS = 3 * 2 * K * H * S
+
+F32 = mybir.dt.float32
+BF16 = mybir.dt.bfloat16
+I32 = mybir.dt.int32
+U32 = mybir.dt.uint32
+U16 = mybir.dt.uint16
+U8 = mybir.dt.uint8
+FP8X4 = mybir.dt.float8_e4m3fn_x4
+ALU = mybir.AluOpType
+ACT = mybir.ActivationFunctionType
+
+P = 128
+PACK = 4
+HALF = S // 2
+LIST_HALF = HALF // 16
+PAGE_HALF = U // 2
+TILE_ORDER = (2, 0, 1, 3)
+
+
+def tile_picked_twqjointbpagex_none_po_kernel(
+    tc, x_words, x_scales, w1_words, w1_scales, w2_words, w2_scales, gs, d_words, d_scales, mem,
+    offs, two, n1, n2, k1, n3, out_0, out_1, out_2,
+):
+    nc = tc.nc
+    with ExitStack() as ctx:
+        sb = ctx.enter_context(tc.tile_pool(name="sb", bufs=1))
+        ps = ctx.enter_context(tc.psum_pool(name="ps", bufs=1))
+
+        def tile(name, shape, dtype):
+            return sb.tile(shape, dtype, name=name, align_bytes=64)
+
+        def load_list(name, src):
+            dst = tile(name, [P, S // 16], U16)
+            nc.sync.dma_start(dst[:], src)
+            return dst
+
+        def load_words(name, src, width):
+            dst = tile(name, [P, width], I32)
+            nc.sync.dma_start(dst[:], src[0].rearrange("p n r -> p (n r)").bitcast(I32))
+            return dst
+
+        def load_scale_rows(dst, src, first):
+            for q in range(4):
+                nc.sync.dma_start(
+                    dst[32 * q + first : 32 * q + first + 4, :].bitcast(I32),
+                    src[0, 4 * q : 4 * q + 4, :].bitcast(I32),
+                )
+
+        def zeroed_bytes(name, width):
+            dst = tile(name, [P, width], U8)
+            nc.vector.memset(dst[:].bitcast(I32), 0)
+            return dst
+
+        def gather(name, table, offsets, tile_dtype, view_dtype):
+            dst = tile(name, [P, S], tile_dtype)
+            nc.vector.tensor_copy(dst[:].bitcast(view_dtype), table[:].bitcast(view_dtype).indirect(offsets[:]))
+            return dst
+
+        def deal(name, src, dtype):
+            dst = tile(name, [P, H], dtype)
+            nc.vector.tensor_copy(
+                dst[:].rearrange("p (t m) -> p m t", t=PACK), src[:].rearrange("p (m t) -> p m t", t=PACK)
+            )
+            return dst
+
+        def product(bank, width, lhs_words, lhs_scales, plane, t, rhs_words, rhs_scales):
+            acc = ps.tile([P, width], F32, name=bank)
+            cols = slice(t * P, (t + 1) * P)
+            nc.tensor.matmul_mx(
+                acc[:], lhsT=lhs_words[:, cols].bitcast(FP8X4), lhsT_scale=lhs_scales[plane:P, cols],
+                rhs=rhs_words.bitcast(FP8X4), rhs_scale=rhs_scales, start=True, stop=True,
+            )
+            return acc
+
+        x_s = zeroed_bytes("x_s", T)
+        w_s = zeroed_bytes("w_s", H)
+        d_s = zeroed_bytes("d_s", G)
+        code_s = zeroed_bytes("code_s", H)
+
+        two_l = load_list("two_l", two)
+        offs_l = load_list("offs_l", offs)
+        x_w = load_words("x_w", x_words, T)
+        w2_w = load_words("w2_w", w2_words, H)
+        load_scale_rows(x_s, x_scales, 0)
+        load_scale_rows(w_s, w2_scales, 0)
+        load_scale_rows(w_s, w1_scales, 4)
+        n2_l = load_list("n2_l", n2)
+        n1_l = load_list("n1_l", n1)
+        w1_w = load_words("w1_w", w1_words, H)
+        gs_t = tile("gs_t", [P, PACK], F32)
+        nc.sync.dma_start(gs_t[:], gs.rearrange("(p t) o -> p (t o)", t=PACK))
+        k1_l = load_list("k1_l", k1)
+        load_scale_rows(d_s, d_scales, 14)
+        n3_l = load_list("n3_l", n3)
+        mem_rows = mem.rearrange("(p t) u -> p t u", t=PACK)
+        page = {}
+        for t in TILE_ORDER:
+            page[t] = tile("page%d" % t, [P, U], F32)
+            nc.sync.dma_start(page[t][:], mem_rows[:, t, :])
+        d_w = load_words("d_w", d_words, G)
+
+        two_w = gather("two_w", x_w, two_l, I32, U32)
+        two_s = gather("two_s", x_s, two_l, U8, U8)
+        w2_dealt = deal("w2_dealt", w2_w, I32)
+        ws_dealt = deal("ws_dealt", w_s, U8)
+        offs_s = gather("offs_s", x_s, offs_l, U8, U8)
+        offs_w = gather("offs_w", x_w, offs_l, I32, U32)
+        w1_dealt = deal("w1_dealt", w1_w, I32)
+
+        d_rows = {}
+        for t in range(PACK):
+            acc = product("bank%d" % t, S, w2_dealt, ws_dealt, 0, t, two_w[:], two_s[:])
+            d_rows[t] = tile("d_rows%d" % t, [P, S], F32)
+            nc.scalar.copy(d_rows[t][:], acc[:])
+
+        picked_s = gather("picked_s", d_s, k1_l, U8, U8)
+
+        halves = [slice(h * HALF, (h + 1) * HALF) for h in range(2)]
+        list_halves = [slice(h * LIST_HALF, (h + 1) * LIST_HALF) for h in range(2)]
+        y_gs = tile("y_gs", [P, PACK, S], F32)
+        for t in range(PACK):
+            acc = product("bank%d" % (PACK + t), S, w1_dealt, ws_dealt, 4, t, offs_w[:], offs_s[:])
+            nc.scalar.activation(y_gs[:, t, :], acc[:], ACT.Copy, scale=gs_t[:, t : t + 1])
+        half_page = {}
+        for t in TILE_ORDER:
+            half_page[t] = tile("half_page%d" % t, [P, U], F32)
+            nc.scalar.activation(half_page[t][:], page[t][:], ACT.Copy, scale=0.5)
+
+        second = tile("second", [P, PACK, S], F32)
+        gap = tile("gap", [P, PACK, S], F32)
+        gate = tile("gate", [P, PACK, S], F32)
+        for t in range(PACK):
+            for h in range(2):
+                nc.vector.tensor_copy(second[:, t, halves[h]], d_rows[t][:].indirect(n2_l[:, list_halves[h]]))
+            for h in range(2):
+                nc.vector.tensor_tensor(
+                    gap[:, t, halves[h]], d_rows[t][:].indirect(n1_l[:, list_halves[h]]),
+                    second[:, t, halves[h]], ALU.subtract,
+                )
+            for h in range(2):
+                nc.scalar.activation(gate[:, t, halves[h]], gap[:, t, halves[h]], ACT.Tanh)
+            if t == 0:
+                picked_s_dealt = deal("picked_s_dealt", picked_s, U8)
+                for q in range(4):
+                    nc.sync.dma_start(
+                        code_s[32 * q : 32 * q + 4, :].bitcast(I32),
+                        picked_s_dealt[32 * q + 14 : 32 * q + 18, :].bitcast(I32),
+                    )
+
+        picked_w = gather("picked_w", d_w, k1_l, I32, U32)
+
+        h_rows = {t: tile("h_rows%d" % t, [P, S], F32) for t in TILE_ORDER}
+        excess = {t: tile("excess%d" % t, [P, S], F32) for t in TILE_ORDER[:-1]}
+        for h in range(2):
+            z = tile("z%d" % h, [P, HALF, PACK], BF16)
+            nc.vector.tensor_tensor(
+                z[:].rearrange("p (c i) t -> p c t i", i=4),
+                y_gs[:, :, halves[h]].rearrange("p t (c i) -> p c t i", i=4),
+                gate[:, :, halves[h]].rearrange("p t (c i) -> p c t i", i=4),
+                ALU.mult,
+            )
+            if h == 0:
+                code_w = deal("code_w", picked_w, I32)
+            z_w = tile("z_w%d" % h, [P, HALF], I32)
+            z_s = tile("z_s%d" % h, [P, HALF], U8)
+            nc.vector.quantize_mx(z_w[:].bitcast(FP8X4), z_s[:], z[:].rearrange("p j t -> p (j t)"))
+            for t in TILE_ORDER:
+                acc = product("bank%d" % (PACK * h + t), HALF, code_w, code_s, 0, t, z_w[:], z_s[:])
+                nc.scalar.activation(h_rows[t][:, halves[h]], acc[:], ACT.Copy, scale=0.0625)
+        for h in range(2):
+            for t in TILE_ORDER[:-1]:
+                nc.vector.tensor_tensor(
+                    excess[t][:, halves[h]], half_page[t][:].indirect(n3_l[:, list_halves[h]]),
+                    h_rows[t][:, halves[h]], ALU.subtract,
+                )
+
+        out_rows = out_0.rearrange("(p t) u -> p t u", t=PACK)
+        rounded = [tile("rounded%d" % c, [P, PAGE_HALF, PACK], BF16) for c in range(2)]
+        first, second_t, third, last = TILE_ORDER
+        lift = {}
+
+        def rectify(t):
+            lift[t] = tile("lift%d" % t, [P, S], F32)
+            nc.scalar.activation(lift[t][:], excess[t][:], ACT.Relu)
+
+        def put(t):
+            nc.vector.tensor_tensor(page[t][:].indirect(n3_l[:]), h_rows[t][:], lift[t][:], ALU.add)
+            nc.sync.dma_start(out_rows[:, t, :], page[t][:])
+
+        def round_out(t):
+            for c in range(2):
+                src = page[t][:, c * PAGE_HALF : (c + 1) * PAGE_HALF]
+                if t == last and c == 0:
+                    nc.vector.tensor_copy(rounded[c][:, :, t], src)
+                else:
+                    nc.scalar.copy(rounded[c][:, :, t], src)
+
+        for t in TILE_ORDER[:-1]:
+            rectify(t)
+        put(first)
+        round_out(first)
+        put(second_t)
+        round_out(second_t)
+        excess[last] = tile("lift%d" % first, [P, S], F32)
+        nc.vector.tensor_tensor(excess[last][:], half_page[last][:].indirect(n3_l[:]), h_rows[last][:], ALU.subtract)
+        rectify(last)
+        put(third)
+        round_out(third)
+        put(last)
+        round_out(last)
+
+        out_words = out_1[0].rearrange("p u r -> p (u r)").bitcast(I32)
+        out_s = tile("out_s", [P, U], U8)
+        for c in range(2):
+            cols = slice(c * PAGE_HALF, (c + 1) * PAGE_HALF)
+            out_w = tile("out_w%d" % c, [P, PAGE_HALF], I32)
+            nc.vector.quantize_mx(out_w[:].bitcast(FP8X4), out_s[:, cols], rounded[c][:].rearrange("p u t -> p (u t)"))
+            nc.sync.dma_start(out_words[:, cols], out_w[:])
+        for q in range(4):
+            queue = nc.sync if q % 2 == 0 else nc.scalar
+            queue.dma_start(out_2[0, 4 * q : 4 * q + 4, :].bitcast(I32), out_s[32 * q : 32 * q + 4, :].bitcast(I32))

@@ -1,6 +1,7 @@
 from contextlib import ExitStack
 
 import concourse.mybir as mybir
+from concourse.masks import make_identity
 
 K, T, S, H, G, U = 512, 1024, 512, 512, 2048, 1024
 FLOPS = 3 * 2 * K * H * S
@@ -19,8 +20,10 @@ P = 128
 PACK = 4
 HALF = S // 2
 LIST_HALF = HALF // 16
-PAGE_HALF = U // 2
+PAGE_PIECES = (slice(0, 512), slice(512, 768), slice(768, 1024))
 TILE_ORDER = (2, 0, 1, 3)
+LEAD = 64
+VECTOR_SHARE = 640
 
 
 def tile_picked_twqjointbpagex_none_po_kernel(
@@ -79,43 +82,46 @@ def tile_picked_twqjointbpagex_none_po_kernel(
             return acc
 
         x_s = zeroed_bytes("x_s", T)
-        w_s = zeroed_bytes("w_s", H)
+        w2_s = zeroed_bytes("w2_s", H)
+        w1_s = zeroed_bytes("w1_s", H)
         d_s = zeroed_bytes("d_s", G)
         code_s = zeroed_bytes("code_s", H)
 
+        identity = tile("identity", [P, P], F32)
+        make_identity(nc, identity[:])
+
         two_l = load_list("two_l", two)
-        offs_l = load_list("offs_l", offs)
         x_w = load_words("x_w", x_words, T)
+        offs_l = load_list("offs_l", offs)
         w2_w = load_words("w2_w", w2_words, H)
-        load_scale_rows(x_s, x_scales, 0)
-        load_scale_rows(w_s, w2_scales, 0)
-        load_scale_rows(w_s, w1_scales, 4)
         n2_l = load_list("n2_l", n2)
         n1_l = load_list("n1_l", n1)
-        w1_w = load_words("w1_w", w1_words, H)
+        k1_l = load_list("k1_l", k1)
         gs_t = tile("gs_t", [P, PACK], F32)
         nc.sync.dma_start(gs_t[:], gs.rearrange("(p t) o -> p (t o)", t=PACK))
-        k1_l = load_list("k1_l", k1)
+        load_scale_rows(x_s, x_scales, 0)
+        load_scale_rows(w2_s, w2_scales, 0)
         load_scale_rows(d_s, d_scales, 14)
+        w1_w = load_words("w1_w", w1_words, H)
+        load_scale_rows(w1_s, w1_scales, 0)
+        d_w = load_words("d_w", d_words, G)
         n3_l = load_list("n3_l", n3)
         mem_rows = mem.rearrange("(p t) u -> p t u", t=PACK)
         page = {}
         for t in TILE_ORDER:
             page[t] = tile("page%d" % t, [P, U], F32)
             nc.sync.dma_start(page[t][:], mem_rows[:, t, :])
-        d_w = load_words("d_w", d_words, G)
 
         two_w = gather("two_w", x_w, two_l, I32, U32)
         two_s = gather("two_s", x_s, two_l, U8, U8)
         w2_dealt = deal("w2_dealt", w2_w, I32)
-        ws_dealt = deal("ws_dealt", w_s, U8)
-        offs_s = gather("offs_s", x_s, offs_l, U8, U8)
-        offs_w = gather("offs_w", x_w, offs_l, I32, U32)
-        w1_dealt = deal("w1_dealt", w1_w, I32)
+        w2_s_dealt = deal("w2_s_dealt", w2_s, U8)
+        offs_s = gather("w2_s", x_s, offs_l, U8, U8)
+        offs_w = gather("w2_w", x_w, offs_l, I32, U32)
 
         d_rows = {}
         for t in range(PACK):
-            acc = product("bank%d" % t, S, w2_dealt, ws_dealt, 0, t, two_w[:], two_s[:])
+            acc = product("bank%d" % t, S, w2_dealt, w2_s_dealt, 0, t, two_w[:], two_s[:])
             d_rows[t] = tile("d_rows%d" % t, [P, S], F32)
             nc.scalar.copy(d_rows[t][:], acc[:])
 
@@ -124,17 +130,19 @@ def tile_picked_twqjointbpagex_none_po_kernel(
         halves = [slice(h * HALF, (h + 1) * HALF) for h in range(2)]
         list_halves = [slice(h * LIST_HALF, (h + 1) * LIST_HALF) for h in range(2)]
         y_gs = tile("y_gs", [P, PACK, S], F32)
+        y_turned = tile("y_turned", [P, PACK, H], F32)
+        for b in range(PACK):
+            acc = product("bank%d" % (PACK + b), H, offs_w, offs_s, 0, b, w1_w[:], w1_s[:])
+            nc.scalar.copy(y_turned[:, b, :], acc[:])
         for t in range(PACK):
-            acc = product("bank%d" % (PACK + t), S, w1_dealt, ws_dealt, 4, t, offs_w[:], offs_s[:])
+            acc = ps.tile([P, S], F32, name="bank%d" % t)
+            for b in range(PACK):
+                nc.tensor.transpose(acc[:, b * P : (b + 1) * P], y_turned[:, b, t:H:PACK], identity[:])
             nc.scalar.activation(y_gs[:, t, :], acc[:], ACT.Copy, scale=gs_t[:, t : t + 1])
-        half_page = {}
-        for t in TILE_ORDER:
-            half_page[t] = tile("half_page%d" % t, [P, U], F32)
-            nc.scalar.activation(half_page[t][:], page[t][:], ACT.Copy, scale=0.5)
 
         second = tile("second", [P, PACK, S], F32)
         gap = tile("gap", [P, PACK, S], F32)
-        gate = tile("gate", [P, PACK, S], F32)
+        gate = tile("y_turned", [P, PACK, S], F32)
         for t in range(PACK):
             for h in range(2):
                 nc.vector.tensor_copy(second[:, t, halves[h]], d_rows[t][:].indirect(n2_l[:, list_halves[h]]))
@@ -156,60 +164,85 @@ def tile_picked_twqjointbpagex_none_po_kernel(
         picked_w = gather("picked_w", d_w, k1_l, I32, U32)
 
         h_rows = {t: tile("h_rows%d" % t, [P, S], F32) for t in TILE_ORDER}
+        twice = {t: tile("twice%d" % t, [P, S], F32) for t in TILE_ORDER}
+        sums = {}
         excess = {t: tile("excess%d" % t, [P, S], F32) for t in TILE_ORDER[:-1]}
-        for h in range(2):
-            z = tile("z%d" % h, [P, HALF, PACK], BF16)
+        code_w = deal("code_w", picked_w, I32)
+        z = [tile("z%d" % h, [P, HALF * PACK], BF16) for h in range(2)]
+
+        def multiply(h, start, stop):
+            cols = slice(h * HALF + start, h * HALF + stop)
             nc.vector.tensor_tensor(
-                z[:].rearrange("p (c i) t -> p c t i", i=4),
-                y_gs[:, :, halves[h]].rearrange("p t (c i) -> p c t i", i=4),
-                gate[:, :, halves[h]].rearrange("p t (c i) -> p c t i", i=4),
+                z[h][:, PACK * start : PACK * stop].rearrange("p (c i t) -> p c t i", i=4, t=PACK),
+                y_gs[:, :, cols].rearrange("p t (c i) -> p c t i", i=4),
+                gate[:, :, cols].rearrange("p t (c i) -> p c t i", i=4),
                 ALU.mult,
             )
-            if h == 0:
-                code_w = deal("code_w", picked_w, I32)
+
+        def doubled(t, h):
+            nc.scalar.activation(twice[t][:, halves[h]], sums[t, h][:], ACT.Copy, scale=0.125)
+
+        def coded_layer(h):
             z_w = tile("z_w%d" % h, [P, HALF], I32)
             z_s = tile("z_s%d" % h, [P, HALF], U8)
-            nc.vector.quantize_mx(z_w[:].bitcast(FP8X4), z_s[:], z[:].rearrange("p j t -> p (j t)"))
+            nc.vector.quantize_mx(z_w[:].bitcast(FP8X4), z_s[:], z[h][:])
             for t in TILE_ORDER:
-                acc = product("bank%d" % (PACK * h + t), HALF, code_w, code_s, 0, t, z_w[:], z_s[:])
-                nc.scalar.activation(h_rows[t][:, halves[h]], acc[:], ACT.Copy, scale=0.0625)
+                sums[t, h] = product("bank%d" % (PACK * (1 - h) + t), HALF, code_w, code_s, 0, t, z_w[:], z_s[:])
+                if t != TILE_ORDER[-1]:
+                    doubled(t, h)
+
+        multiply(0, 0, HALF)
+        multiply(1, 0, LEAD)
+        coded_layer(0)
+        multiply(1, LEAD, HALF)
+        coded_layer(1)
         for h in range(2):
             for t in TILE_ORDER[:-1]:
                 nc.vector.tensor_tensor(
-                    excess[t][:, halves[h]], half_page[t][:].indirect(n3_l[:, list_halves[h]]),
-                    h_rows[t][:, halves[h]], ALU.subtract,
+                    excess[t][:, halves[h]], page[t][:].indirect(n3_l[:, list_halves[h]]),
+                    twice[t][:, halves[h]], ALU.subtract,
                 )
 
         out_rows = out_0.rearrange("(p t) u -> p t u", t=PACK)
-        rounded = [tile("rounded%d" % c, [P, PAGE_HALF, PACK], BF16) for c in range(2)]
+        rounded = tile("rounded", [P, U * PACK], BF16)
+        rounded_by_row = rounded[:].rearrange("p (u t) -> p u t", t=PACK)
         first, second_t, third, last = TILE_ORDER
         lift = {}
 
         def rectify(t):
             lift[t] = tile("lift%d" % t, [P, S], F32)
-            nc.scalar.activation(lift[t][:], excess[t][:], ACT.Relu)
+            nc.scalar.activation(lift[t][:], excess[t][:], ACT.Relu, scale=0.5)
 
         def put(t):
             nc.vector.tensor_tensor(page[t][:].indirect(n3_l[:]), h_rows[t][:], lift[t][:], ALU.add)
             nc.sync.dma_start(out_rows[:, t, :], page[t][:])
 
         def round_out(t):
-            for c in range(2):
-                src = page[t][:, c * PAGE_HALF : (c + 1) * PAGE_HALF]
-                if t == last and c == 0:
-                    nc.vector.tensor_copy(rounded[c][:, :, t], src)
-                else:
-                    nc.scalar.copy(rounded[c][:, :, t], src)
+            if t != last:
+                nc.scalar.copy(rounded_by_row[:, :, t], page[t][:])
+                return
+            for cols in (slice(0, 512), slice(512, VECTOR_SHARE)):
+                nc.vector.tensor_copy(rounded_by_row[:, cols, t], page[t][:, cols])
+            nc.scalar.copy(rounded_by_row[:, VECTOR_SHARE:U, t], page[t][:, VECTOR_SHARE:U])
+
+        def plain_h(t):
+            for h in range(2):
+                nc.scalar.activation(h_rows[t][:, halves[h]], sums[t, h][:], ACT.Copy, scale=0.0625)
 
         for t in TILE_ORDER[:-1]:
+            plain_h(t)
             rectify(t)
+            if t == first:
+                for h in range(2):
+                    doubled(last, h)
+        plain_h(last)
         put(first)
         round_out(first)
+        excess[last] = tile("lift%d" % first, [P, S], F32)
+        nc.vector.tensor_tensor(excess[last][:], page[last][:].indirect(n3_l[:]), twice[last][:], ALU.subtract)
+        rectify(last)
         put(second_t)
         round_out(second_t)
-        excess[last] = tile("lift%d" % first, [P, S], F32)
-        nc.vector.tensor_tensor(excess[last][:], half_page[last][:].indirect(n3_l[:]), h_rows[last][:], ALU.subtract)
-        rectify(last)
         put(third)
         round_out(third)
         put(last)
@@ -217,10 +250,10 @@ def tile_picked_twqjointbpagex_none_po_kernel(
 
         out_words = out_1[0].rearrange("p u r -> p (u r)").bitcast(I32)
         out_s = tile("out_s", [P, U], U8)
-        for c in range(2):
-            cols = slice(c * PAGE_HALF, (c + 1) * PAGE_HALF)
-            out_w = tile("out_w%d" % c, [P, PAGE_HALF], I32)
-            nc.vector.quantize_mx(out_w[:].bitcast(FP8X4), out_s[:, cols], rounded[c][:].rearrange("p u t -> p (u t)"))
+        for c in range(3):
+            cols = PAGE_PIECES[c]
+            out_w = tile("out_w%d" % c, [P, cols.stop - cols.start], I32)
+            nc.vector.quantize_mx(out_w[:].bitcast(FP8X4), out_s[:, cols], rounded[:, PACK * cols.start : PACK * cols.stop])
             nc.sync.dma_start(out_words[:, cols], out_w[:])
         for q in range(4):
             queue = nc.sync if q % 2 == 0 else nc.scalar

@@ -23,7 +23,6 @@ LIST_HALF = HALF // 16
 PAGE_PIECES = (slice(0, 512), slice(512, 768), slice(768, 1024))
 TILE_ORDER = (2, 0, 1, 3)
 LEAD = 64
-VECTOR_SHARE = 640
 
 
 def tile_picked_twqjointbpagex_none_po_kernel(
@@ -55,9 +54,9 @@ def tile_picked_twqjointbpagex_none_po_kernel(
                     src[0, 4 * q : 4 * q + 4, :].bitcast(I32),
                 )
 
-        def zeroed_bytes(name, width):
+        def zeroed_bytes(name, width, engine):
             dst = tile(name, [P, width], U8)
-            nc.vector.memset(dst[:].bitcast(I32), 0)
+            engine.memset(dst[:].bitcast(I32), 0)
             return dst
 
         def gather(name, table, offsets, tile_dtype, view_dtype):
@@ -81,29 +80,42 @@ def tile_picked_twqjointbpagex_none_po_kernel(
             )
             return acc
 
-        x_s = zeroed_bytes("x_s", T)
-        w2_s = zeroed_bytes("w2_s", H)
-        w1_s = zeroed_bytes("w1_s", H)
-        d_s = zeroed_bytes("d_s", G)
-        code_s = zeroed_bytes("code_s", H)
+        def move_scale_rows(dst, src, first):
+            for q in range(4):
+                nc.sync.dma_start(
+                    dst[32 * q : 32 * q + 4, :].bitcast(I32), src[32 * q + first : 32 * q + first + 4, :].bitcast(I32)
+                )
+
+        x_s_top = tile("x_s_top", [P, T], U8)
+        for q in range(4):
+            nc.vector.memset(x_s_top[32 * q : 32 * q + 28, :].bitcast(I32), 0)
+        x_s = zeroed_bytes("x_s", T, nc.vector)
+        w2_s = zeroed_bytes("w2_s", H, nc.vector)
+        offs_s = zeroed_bytes("offs_s", S, nc.gpsimd)
+        d_s = zeroed_bytes("d_s", G, nc.gpsimd)
+        w1_s = zeroed_bytes("w1_s", H, nc.gpsimd)
+        code_s = zeroed_bytes("code_s", H, nc.gpsimd)
 
         identity = tile("identity", [P, P], F32)
         make_identity(nc, identity[:])
 
+        offs_l = load_list("offs_l", offs)
+        load_scale_rows(x_s_top, x_scales, 28)
         two_l = load_list("two_l", two)
         x_w = load_words("x_w", x_words, T)
-        offs_l = load_list("offs_l", offs)
         w2_w = load_words("w2_w", w2_words, H)
-        n2_l = load_list("n2_l", n2)
-        n1_l = load_list("n1_l", n1)
-        k1_l = load_list("k1_l", k1)
-        gs_t = tile("gs_t", [P, PACK], F32)
-        nc.sync.dma_start(gs_t[:], gs.rearrange("(p t) o -> p (t o)", t=PACK))
         load_scale_rows(x_s, x_scales, 0)
         load_scale_rows(w2_s, w2_scales, 0)
+        k1_l = load_list("k1_l", k1)
         load_scale_rows(d_s, d_scales, 14)
+        n2_l = load_list("n2_l", n2)
+        n1_l = load_list("n1_l", n1)
+        offs_s_top = gather("offs_s_top", x_s_top, offs_l, U8, U8)
+        move_scale_rows(offs_s, offs_s_top, 28)
         w1_w = load_words("w1_w", w1_words, H)
         load_scale_rows(w1_s, w1_scales, 0)
+        gs_t = tile("gs_t", [P, PACK], F32)
+        nc.sync.dma_start(gs_t[:], gs.rearrange("(p t) o -> p (t o)", t=PACK))
         d_w = load_words("d_w", d_words, G)
         n3_l = load_list("n3_l", n3)
         mem_rows = mem.rearrange("(p t) u -> p t u", t=PACK)
@@ -116,8 +128,7 @@ def tile_picked_twqjointbpagex_none_po_kernel(
         two_s = gather("two_s", x_s, two_l, U8, U8)
         w2_dealt = deal("w2_dealt", w2_w, I32)
         w2_s_dealt = deal("w2_s_dealt", w2_s, U8)
-        offs_s = gather("w2_s", x_s, offs_l, U8, U8)
-        offs_w = gather("w2_w", x_w, offs_l, I32, U32)
+        offs_w = gather("w2_s", x_w, offs_l, I32, U32)
 
         d_rows = {}
         for t in range(PACK):
@@ -155,16 +166,20 @@ def tile_picked_twqjointbpagex_none_po_kernel(
                 nc.scalar.activation(gate[:, t, halves[h]], gap[:, t, halves[h]], ACT.Tanh)
             if t == 0:
                 picked_s_dealt = deal("picked_s_dealt", picked_s, U8)
-                for q in range(4):
-                    nc.sync.dma_start(
-                        code_s[32 * q : 32 * q + 4, :].bitcast(I32),
-                        picked_s_dealt[32 * q + 14 : 32 * q + 18, :].bitcast(I32),
-                    )
+                move_scale_rows(code_s, picked_s_dealt, 14)
+
+        half_page = {}
+
+        def halve(t, name):
+            half_page[t] = tile(name, [P, U], F32)
+            nc.scalar.activation(half_page[t][:], page[t][:], ACT.Copy, scale=0.5)
+
+        for t in TILE_ORDER[:-1]:
+            halve(t, "half_page%d" % t)
 
         picked_w = gather("picked_w", d_w, k1_l, I32, U32)
 
         h_rows = {t: tile("h_rows%d" % t, [P, S], F32) for t in TILE_ORDER}
-        twice = {t: tile("twice%d" % t, [P, S], F32) for t in TILE_ORDER}
         sums = {}
         excess = {t: tile("excess%d" % t, [P, S], F32) for t in TILE_ORDER[:-1]}
         code_w = deal("code_w", picked_w, I32)
@@ -179,8 +194,8 @@ def tile_picked_twqjointbpagex_none_po_kernel(
                 ALU.mult,
             )
 
-        def doubled(t, h):
-            nc.scalar.activation(twice[t][:, halves[h]], sums[t, h][:], ACT.Copy, scale=0.125)
+        def scale_out(t, h):
+            nc.scalar.activation(h_rows[t][:, halves[h]], sums[t, h][:], ACT.Copy, scale=0.0625)
 
         def coded_layer(h):
             z_w = tile("z_w%d" % h, [P, HALF], I32)
@@ -189,7 +204,7 @@ def tile_picked_twqjointbpagex_none_po_kernel(
             for t in TILE_ORDER:
                 sums[t, h] = product("bank%d" % (PACK * (1 - h) + t), HALF, code_w, code_s, 0, t, z_w[:], z_s[:])
                 if t != TILE_ORDER[-1]:
-                    doubled(t, h)
+                    scale_out(t, h)
 
         multiply(0, 0, HALF)
         multiply(1, 0, LEAD)
@@ -199,47 +214,40 @@ def tile_picked_twqjointbpagex_none_po_kernel(
         for h in range(2):
             for t in TILE_ORDER[:-1]:
                 nc.vector.tensor_tensor(
-                    excess[t][:, halves[h]], page[t][:].indirect(n3_l[:, list_halves[h]]),
-                    twice[t][:, halves[h]], ALU.subtract,
+                    excess[t][:, halves[h]], half_page[t][:].indirect(n3_l[:, list_halves[h]]),
+                    h_rows[t][:, halves[h]], ALU.subtract,
                 )
 
         out_rows = out_0.rearrange("(p t) u -> p t u", t=PACK)
-        rounded = tile("rounded", [P, U * PACK], BF16)
-        rounded_by_row = rounded[:].rearrange("p (u t) -> p u t", t=PACK)
+        rounded = [tile("rounded%d" % c, [P, cols.stop - cols.start, PACK], BF16) for c, cols in enumerate(PAGE_PIECES)]
         first, second_t, third, last = TILE_ORDER
         lift = {}
 
         def rectify(t):
             lift[t] = tile("lift%d" % t, [P, S], F32)
-            nc.scalar.activation(lift[t][:], excess[t][:], ACT.Relu, scale=0.5)
+            nc.scalar.activation(lift[t][:], excess[t][:], ACT.Relu)
 
         def put(t):
             nc.vector.tensor_tensor(page[t][:].indirect(n3_l[:]), h_rows[t][:], lift[t][:], ALU.add)
             nc.sync.dma_start(out_rows[:, t, :], page[t][:])
 
         def round_out(t):
-            if t != last:
-                nc.scalar.copy(rounded_by_row[:, :, t], page[t][:])
-                return
-            for cols in (slice(0, 512), slice(512, VECTOR_SHARE)):
-                nc.vector.tensor_copy(rounded_by_row[:, cols, t], page[t][:, cols])
-            nc.scalar.copy(rounded_by_row[:, VECTOR_SHARE:U, t], page[t][:, VECTOR_SHARE:U])
-
-        def plain_h(t):
-            for h in range(2):
-                nc.scalar.activation(h_rows[t][:, halves[h]], sums[t, h][:], ACT.Copy, scale=0.0625)
+            for c, cols in enumerate(PAGE_PIECES):
+                if t == last and c == 0:
+                    nc.vector.tensor_copy(rounded[c][:, :, t], page[t][:, cols])
+                else:
+                    nc.scalar.copy(rounded[c][:, :, t], page[t][:, cols])
 
         for t in TILE_ORDER[:-1]:
-            plain_h(t)
             rectify(t)
             if t == first:
+                halve(last, "excess%d" % first)
                 for h in range(2):
-                    doubled(last, h)
-        plain_h(last)
+                    scale_out(last, h)
         put(first)
         round_out(first)
         excess[last] = tile("lift%d" % first, [P, S], F32)
-        nc.vector.tensor_tensor(excess[last][:], page[last][:].indirect(n3_l[:]), twice[last][:], ALU.subtract)
+        nc.vector.tensor_tensor(excess[last][:], half_page[last][:].indirect(n3_l[:]), h_rows[last][:], ALU.subtract)
         rectify(last)
         put(second_t)
         round_out(second_t)
@@ -250,10 +258,10 @@ def tile_picked_twqjointbpagex_none_po_kernel(
 
         out_words = out_1[0].rearrange("p u r -> p (u r)").bitcast(I32)
         out_s = tile("out_s", [P, U], U8)
-        for c in range(3):
+        for c in (1, 0, 2):
             cols = PAGE_PIECES[c]
             out_w = tile("out_w%d" % c, [P, cols.stop - cols.start], I32)
-            nc.vector.quantize_mx(out_w[:].bitcast(FP8X4), out_s[:, cols], rounded[:, PACK * cols.start : PACK * cols.stop])
+            nc.vector.quantize_mx(out_w[:].bitcast(FP8X4), out_s[:, cols], rounded[c][:].rearrange("p u t -> p (u t)"))
             nc.sync.dma_start(out_words[:, cols], out_w[:])
         for q in range(4):
             queue = nc.sync if q % 2 == 0 else nc.scalar

@@ -66,8 +66,9 @@ def tile_picked_twqjointbpagex_none_po_kernel(
 
         def deal(name, src, dtype):
             dst = tile(name, [P, H], dtype)
+            walk = "p t m" if dtype == U8 else "p m t"
             nc.vector.tensor_copy(
-                dst[:].rearrange("p (t m) -> p m t", t=PACK), src[:].rearrange("p (m t) -> p m t", t=PACK)
+                dst[:].rearrange("p (t m) -> " + walk, t=PACK), src[:].rearrange("p (m t) -> " + walk, t=PACK)
             )
             return dst
 
@@ -144,11 +145,13 @@ def tile_picked_twqjointbpagex_none_po_kernel(
         y_turned = tile("y_turned", [P, PACK, H], F32)
         for b in range(PACK):
             acc = product("bank%d" % (PACK + b), H, offs_w, offs_s, 0, b, w1_w[:], w1_s[:])
-            nc.scalar.copy(y_turned[:, b, :], acc[:])
+            nc.scalar.copy(
+                y_turned[:, b, :].rearrange("j (t m) -> j t m", t=PACK), acc[:].rearrange("j (m t) -> j t m", t=PACK)
+            )
         for t in range(PACK):
             acc = ps.tile([P, S], F32, name="bank%d" % t)
             for b in range(PACK):
-                nc.tensor.transpose(acc[:, b * P : (b + 1) * P], y_turned[:, b, t:H:PACK], identity[:])
+                nc.tensor.transpose(acc[:, b * P : (b + 1) * P], y_turned[:, b, t * P : (t + 1) * P], identity[:])
             nc.scalar.activation(y_gs[:, t, :], acc[:], ACT.Copy, scale=gs_t[:, t : t + 1])
 
         second = tile("second", [P, PACK, S], F32)

from contextlib import ExitStack

import concourse.mybir as mybir
from concourse.masks import make_identity

K, T, S, H, G, U = 512, 1024, 512, 512, 2048, 1024
FLOPS = 3 * 2 * K * H * S

F32 = mybir.dt.float32
BF16 = mybir.dt.bfloat16
I32 = mybir.dt.int32
U32 = mybir.dt.uint32
U16 = mybir.dt.uint16
U8 = mybir.dt.uint8
FP8X4 = mybir.dt.float8_e4m3fn_x4
ALU = mybir.AluOpType
ACT = mybir.ActivationFunctionType

P = 128
PACK = 4
HALF = S // 2
LIST_HALF = HALF // 16
PAGE_PIECES = (slice(0, 512), slice(512, 768), slice(768, 1024))
TILE_ORDER = (2, 0, 1, 3)
LEAD = 64


def tile_picked_twqjointbpagex_none_po_kernel(
    tc, x_words, x_scales, w1_words, w1_scales, w2_words, w2_scales, gs, d_words, d_scales, mem,
    offs, two, n1, n2, k1, n3, out_0, out_1, out_2,
):
    nc = tc.nc
    with ExitStack() as ctx:
        sb = ctx.enter_context(tc.tile_pool(name="sb", bufs=1))
        ps = ctx.enter_context(tc.psum_pool(name="ps", bufs=1))

        def tile(name, shape, dtype):
            return sb.tile(shape, dtype, name=name, align_bytes=64)

        def load_list(name, src):
            dst = tile(name, [P, S // 16], U16)
            nc.sync.dma_start(dst[:], src)
            return dst

        def load_words(name, src, width):
            dst = tile(name, [P, width], I32)
            nc.sync.dma_start(dst[:], src[0].rearrange("p n r -> p (n r)").bitcast(I32))
            return dst

        def load_scale_rows(dst, src, first):
            for q in range(4):
                nc.sync.dma_start(
                    dst[32 * q + first : 32 * q + first + 4, :].bitcast(I32),
                    src[0, 4 * q : 4 * q + 4, :].bitcast(I32),
                )

        def zeroed_bytes(name, width, engine):
            dst = tile(name, [P, width], U8)
            engine.memset(dst[:].bitcast(I32), 0)
            return dst

        def gather(name, table, offsets, tile_dtype, view_dtype):
            dst = tile(name, [P, S], tile_dtype)
            nc.vector.tensor_copy(dst[:].bitcast(view_dtype), table[:].bitcast(view_dtype).indirect(offsets[:]))
            return dst

        def deal(name, src, dtype):
            dst = tile(name, [P, H], dtype)
            walk = "p t m" if dtype == U8 else "p m t"
            nc.vector.tensor_copy(
                dst[:].rearrange("p (t m) -> " + walk, t=PACK), src[:].rearrange("p (m t) -> " + walk, t=PACK)
            )
            return dst

        def product(bank, width, lhs_words, lhs_scales, plane, t, rhs_words, rhs_scales):
            acc = ps.tile([P, width], F32, name=bank)
            cols = slice(t * P, (t + 1) * P)
            nc.tensor.matmul_mx(
                acc[:], lhsT=lhs_words[:, cols].bitcast(FP8X4), lhsT_scale=lhs_scales[plane:P, cols],
                rhs=rhs_words.bitcast(FP8X4), rhs_scale=rhs_scales, start=True, stop=True,
            )
            return acc

        def move_scale_rows(dst, src, first):
            for q in range(4):
                nc.sync.dma_start(
                    dst[32 * q : 32 * q + 4, :].bitcast(I32), src[32 * q + first : 32 * q + first + 4, :].bitcast(I32)
                )

        x_s_top = tile("x_s_top", [P, T], U8)
        for q in range(4):
            nc.vector.memset(x_s_top[32 * q : 32 * q + 28, :].bitcast(I32), 0)
        x_s = zeroed_bytes("x_s", T, nc.vector)
        w2_s = zeroed_bytes("w2_s", H, nc.vector)
        offs_s = zeroed_bytes("offs_s", S, nc.gpsimd)
        d_s = zeroed_bytes("d_s", G, nc.gpsimd)
        w1_s = zeroed_bytes("w1_s", H, nc.gpsimd)
        code_s = zeroed_bytes("code_s", H, nc.gpsimd)

        identity = tile("identity", [P, P], F32)
        make_identity(nc, identity[:])

        offs_l = load_list("offs_l", offs)
        load_scale_rows(x_s_top, x_scales, 28)
        two_l = load_list("two_l", two)
        x_w = load_words("x_w", x_words, T)
        w2_w = load_words("w2_w", w2_words, H)
        load_scale_rows(x_s, x_scales, 0)
        load_scale_rows(w2_s, w2_scales, 0)
        k1_l = load_list("k1_l", k1)
        load_scale_rows(d_s, d_scales, 14)
        n2_l = load_list("n2_l", n2)
        n1_l = load_list("n1_l", n1)
        offs_s_top = gather("offs_s_top", x_s_top, offs_l, U8, U8)
        move_scale_rows(offs_s, offs_s_top, 28)
        w1_w = load_words("w1_w", w1_words, H)
        load_scale_rows(w1_s, w1_scales, 0)
        gs_t = tile("gs_t", [P, PACK], F32)
        nc.sync.dma_start(gs_t[:], gs.rearrange("(p t) o -> p (t o)", t=PACK))
        d_w = load_words("d_w", d_words, G)
        n3_l = load_list("n3_l", n3)
        mem_rows = mem.rearrange("(p t) u -> p t u", t=PACK)
        page = {}
        for t in TILE_ORDER:
            page[t] = tile("page%d" % t, [P, U], F32)
            nc.sync.dma_start(page[t][:], mem_rows[:, t, :])

        two_w = gather("two_w", x_w, two_l, I32, U32)
        two_s = gather("two_s", x_s, two_l, U8, U8)
        w2_dealt = deal("w2_dealt", w2_w, I32)
        w2_s_dealt = deal("w2_s_dealt", w2_s, U8)
        offs_w = gather("w2_s", x_w, offs_l, I32, U32)

        d_rows = {}
        for t in range(PACK):
            acc = product("bank%d" % t, S, w2_dealt, w2_s_dealt, 0, t, two_w[:], two_s[:])
            d_rows[t] = tile("d_rows%d" % t, [P, S], F32)
            nc.scalar.copy(d_rows[t][:], acc[:])

        picked_s = gather("picked_s", d_s, k1_l, U8, U8)

        halves = [slice(h * HALF, (h + 1) * HALF) for h in range(2)]
        list_halves = [slice(h * LIST_HALF, (h + 1) * LIST_HALF) for h in range(2)]
        y_gs = tile("y_gs", [P, PACK, S], F32)
        y_turned = tile("y_turned", [P, PACK, H], F32)
        for b in range(PACK):
            acc = product("bank%d" % (PACK + b), H, offs_w, offs_s, 0, b, w1_w[:], w1_s[:])
            nc.scalar.copy(
                y_turned[:, b, :].rearrange("j (t m) -> j t m", t=PACK), acc[:].rearrange("j (m t) -> j t m", t=PACK)
            )
        for t in range(PACK):
            acc = ps.tile([P, S], F32, name="bank%d" % t)
            for b in range(PACK):
                nc.tensor.transpose(acc[:, b * P : (b + 1) * P], y_turned[:, b, t * P : (t + 1) * P], identity[:])
            nc.scalar.activation(y_gs[:, t, :], acc[:], ACT.Copy, scale=gs_t[:, t : t + 1])

        second = tile("second", [P, PACK, S], F32)
        gap = tile("gap", [P, PACK, S], F32)
        gate = tile("y_turned", [P, PACK, S], F32)
        for t in range(PACK):
            for h in range(2):
                nc.vector.tensor_copy(second[:, t, halves[h]], d_rows[t][:].indirect(n2_l[:, list_halves[h]]))
            for h in range(2):
                nc.vector.tensor_tensor(
                    gap[:, t, halves[h]], d_rows[t][:].indirect(n1_l[:, list_halves[h]]),
                    second[:, t, halves[h]], ALU.subtract,
                )
            for h in range(2):
                nc.scalar.activation(gate[:, t, halves[h]], gap[:, t, halves[h]], ACT.Tanh)
            if t == 0:
                picked_s_dealt = deal("picked_s_dealt", picked_s, U8)
                move_scale_rows(code_s, picked_s_dealt, 14)

        half_page = {}

        def halve(t, name):
            half_page[t] = tile(name, [P, U], F32)
            nc.scalar.activation(half_page[t][:], page[t][:], ACT.Copy, scale=0.5)

        for t in TILE_ORDER[:-1]:
            halve(t, "half_page%d" % t)

        picked_w = gather("picked_w", d_w, k1_l, I32, U32)

        h_rows = {t: tile("h_rows%d" % t, [P, S], F32) for t in TILE_ORDER}
        sums = {}
        excess = {t: tile("excess%d" % t, [P, S], F32) for t in TILE_ORDER[:-1]}
        code_w = deal("code_w", picked_w, I32)
        z = [tile("z%d" % h, [P, HALF * PACK], BF16) for h in range(2)]

        def multiply(h, start, stop):
            cols = slice(h * HALF + start, h * HALF + stop)
            nc.vector.tensor_tensor(
                z[h][:, PACK * start : PACK * stop].rearrange("p (c i t) -> p c t i", i=4, t=PACK),
                y_gs[:, :, cols].rearrange("p t (c i) -> p c t i", i=4),
                gate[:, :, cols].rearrange("p t (c i) -> p c t i", i=4),
                ALU.mult,
            )

        def scale_out(t, h):
            nc.scalar.activation(h_rows[t][:, halves[h]], sums[t, h][:], ACT.Copy, scale=0.0625)

        def coded_layer(h):
            z_w = tile("z_w%d" % h, [P, HALF], I32)
            z_s = tile("z_s%d" % h, [P, HALF], U8)
            nc.vector.quantize_mx(z_w[:].bitcast(FP8X4), z_s[:], z[h][:])
            for t in TILE_ORDER:
                sums[t, h] = product("bank%d" % (PACK * (1 - h) + t), HALF, code_w, code_s, 0, t, z_w[:], z_s[:])
                if t != TILE_ORDER[-1]:
                    scale_out(t, h)

        multiply(0, 0, HALF)
        multiply(1, 0, LEAD)
        coded_layer(0)
        multiply(1, LEAD, HALF)
        coded_layer(1)
        for h in range(2):
            for t in TILE_ORDER[:-1]:
                nc.vector.tensor_tensor(
                    excess[t][:, halves[h]], half_page[t][:].indirect(n3_l[:, list_halves[h]]),
                    h_rows[t][:, halves[h]], ALU.subtract,
                )

        out_rows = out_0.rearrange("(p t) u -> p t u", t=PACK)
        rounded = [tile("rounded%d" % c, [P, cols.stop - cols.start, PACK], BF16) for c, cols in enumerate(PAGE_PIECES)]
        first, second_t, third, last = TILE_ORDER
        lift = {}

        def rectify(t):
            lift[t] = tile("lift%d" % t, [P, S], F32)
            nc.scalar.activation(lift[t][:], excess[t][:], ACT.Relu)

        def put(t):
            nc.vector.tensor_tensor(page[t][:].indirect(n3_l[:]), h_rows[t][:], lift[t][:], ALU.add)
            nc.sync.dma_start(out_rows[:, t, :], page[t][:])

        def round_out(t):
            for c, cols in enumerate(PAGE_PIECES):
                if t == last and c == 0:
                    nc.vector.tensor_copy(rounded[c][:, :, t], page[t][:, cols])
                else:
                    nc.scalar.copy(rounded[c][:, :, t], page[t][:, cols])

        for t in TILE_ORDER[:-1]:
            rectify(t)
            if t == first:
                halve(last, "excess%d" % first)
                for h in range(2):
                    scale_out(last, h)
        put(first)
        round_out(first)
        excess[last] = tile("lift%d" % first, [P, S], F32)
        nc.vector.tensor_tensor(excess[last][:], half_page[last][:].indirect(n3_l[:]), h_rows[last][:], ALU.subtract)
        rectify(last)
        put(second_t)
        round_out(second_t)
        put(third)
        round_out(third)
        put(last)
        round_out(last)

        out_words = out_1[0].rearrange("p u r -> p (u r)").bitcast(I32)
        out_s = tile("out_s", [P, U], U8)
        for c in (1, 0, 2):
            cols = PAGE_PIECES[c]
            out_w = tile("out_w%d" % c, [P, cols.stop - cols.start], I32)
            nc.vector.quantize_mx(out_w[:].bitcast(FP8X4), out_s[:, cols], rounded[c][:].rearrange("p u t -> p (u t)"))
            nc.sync.dma_start(out_words[:, cols], out_w[:])
        for q in range(4):
            queue = nc.sync if q % 2 == 0 else nc.scalar
            queue.dma_start(out_2[0, 4 * q : 4 * q + 4, :].bitcast(I32), out_s[32 * q : 32 * q + 4, :].bitcast(I32))
